import numpy as np
import ml_dtypes


def mxq(x, axis, fmt="e4m3"):
    dtype, down = {"e4m3": (ml_dtypes.float8_e4m3fn, 7), "e5m2": (ml_dtypes.float8_e5m2, 14)}[fmt]
    v = np.moveaxis(np.asarray(x, np.float32).astype(ml_dtypes.bfloat16).astype(np.float64), axis, -1)
    blocks = v.reshape(v.shape[:-1] + (-1, 32))
    amax = np.abs(blocks).max(-1, keepdims=True)
    byte = np.maximum(np.where(amax > 0, np.frexp(amax)[1] - 1 + 127, 0) - down, 1)
    scale = np.exp2(byte - 127.0)
    codes = (blocks / scale).astype(np.float32).astype(dtype).astype(np.float64)
    return np.moveaxis((codes * scale).reshape(v.shape), -1, axis)


WIDE = False


def mx_kscale(k):
    if not WIDE:
        return np.ones(k)
    levels = np.array([30, -30])
    if k % 512:
        return np.exp2(np.random.permutation(np.resize(levels, k // 32))).repeat(32)
    a = np.empty((k // 512, 16))
    for p in range(k // 512):
        a[p, :8] = np.random.permutation(np.resize(levels, 8))
        for g in range(8):
            far = levels[np.abs(levels - a[p, g]) >= 10]
            a[p, g + 8] = far[np.random.randint(len(far))]
    return np.exp2(a.ravel()).repeat(32)


def f64(x):
    return np.asarray(x).astype(np.float64)


def striped(idx):
    return np.tile(np.asarray(idx).reshape(-1, 16).T, (8, 1)).astype(np.uint16)


def unstriped(offs):
    return offs[:16].T.reshape(-1).astype(np.int64)


E2M1 = np.array([0.0, 0.5, 1.0, 1.5, 2.0, 3.0, 4.0, 6.0, -0.0, -0.5, -1.0, -1.5, -2.0, -3.0, -4.0, -6.0])


def pack_weight(w, fmt):
    k, n = w.shape
    w = f64(np.asarray(w, np.float32).astype(ml_dtypes.bfloat16)).reshape(k // 32, 32, n)
    amax = np.abs(w).max(1)
    if fmt in ("e4m3", "e5m2"):
        byte = np.frexp(amax)[1] - 1 + 127 - (7 if fmt == "e4m3" else 14)
    else:
        mant, ex = np.frexp(amax / 6.0)
        byte = np.where(mant > 0.5, ex, ex - 1) + 127
    byte = np.clip(np.where(amax > 0, byte, 1), 1, 254)
    scaled = (w * np.exp2(127.0 - byte)[:, None, :]).reshape(k, n).astype(np.float32)
    by_word = np.ascontiguousarray(scaled.reshape(k // 512, 128, 4, n).transpose(0, 1, 3, 2))
    if fmt in ("e4m3", "e5m2"):
        words = by_word.astype(ml_dtypes.float8_e4m3fn if fmt == "e4m3" else ml_dtypes.float8_e5m2).view(np.uint8)
    else:
        c = by_word.astype(ml_dtypes.float4_e2m1fn).view(np.uint8) & 0xF
        words = (c[..., 0::2] | (c[..., 1::2] << 4)).reshape(k // 512, 128, 2 * n)
    return np.ascontiguousarray(words), np.ascontiguousarray(byte.astype(np.uint8).reshape(k // 512, 16, n))


def unpack_weight(words, scales, fmt):
    g, _, n = scales.shape
    words = np.ascontiguousarray(words).reshape(g, 128, n, -1)
    if fmt in ("e4m3", "e5m2"):
        vals = words.view(ml_dtypes.float8_e4m3fn if fmt == "e4m3" else ml_dtypes.float8_e5m2).astype(np.float64)
    else:
        nib = np.empty((g, 128, n, 4), np.uint8)
        nib[..., 0::2] = words & 0xF
        nib[..., 1::2] = words >> 4
        vals = E2M1[nib]
    vals = vals * np.repeat(np.exp2(scales.astype(np.float64) - 127.0), 8, axis=1)[..., None]
    return vals.transpose(0, 1, 3, 2).reshape(g * 512, n)


K, T, J, R, O, N, S = 512, 1024, 256, 512, 128, 256, 1024


def setup_inputs():
    n = np.random.standard_normal
    idx = np.random.permutation(T)[:J]
    idx2 = np.random.permutation(J)[:O]
    idx3 = np.random.permutation(J)[:O]
    idx4 = np.random.permutation(S)[:N]
    fk = mx_kscale(K)
    fr = mx_kscale(R)
    xtp = pack_weight(n((K, T)) / fk[:, None], "e2m1")
    wp = pack_weight(n((K, R)) * 1 / np.sqrt(K) * fk[:, None], "e5m2")
    vsp = pack_weight(n((R, S)) * 1 / np.sqrt(R) / fr[:, None], "e4m3")
    return {
        "xt_words": xtp[0],
        "xt_scales": xtp[1],
        "w_words": wp[0],
        "w_scales": wp[1],
        "sa": (np.random.uniform(0.5, 1.6, (R, 1)) * fr[:, None]).astype(np.float32),
        "sb": (np.random.uniform(0.5, 1.6, (R, 1)) * fr[:, None]).astype(np.float32),
        "vs_words": vsp[0],
        "vs_scales": vsp[1],
        "offs": striped(idx),
        "offs2": striped(idx2),
        "offs3": striped(idx3),
        "offs4": striped(idx4),
    }


def reference(xt_words, xt_scales, w_words, w_scales, sa, sb, vs_words, vs_scales, offs, offs2, offs3, offs4):
    idx = unstriped(offs)
    idx2 = unstriped(offs2)
    idx3 = unstriped(offs3)
    idx4 = unstriped(offs4)
    xtu = unpack_weight(xt_words, xt_scales, "e2m1")
    wu = unpack_weight(w_words, w_scales, "e5m2")
    vsu = unpack_weight(vs_words, vs_scales, "e4m3")
    xtidxg = xtu[:, idx]
    a = wu.T @ xtidxg
    hid = np.maximum(a[:, idx2] * f64(sa), a[:, idx3] * f64(sb))
    vsidx4g = vsu[:, idx4]
    hidq = mxq(hid, 0, "e5m2")
    y = vsidx4g.T @ hidq
    return y

@@ -1,0 +1,166 @@
+from contextlib import ExitStack
+
+import concourse.mybir as mybir
+
+K, T, J, R, O, N, S = 512, 1024, 256, 512, 128, 256, 1024
+FLOPS = 2 * K * R * J + 2 * R * N * O
+
+F32 = mybir.dt.float32
+BF16 = mybir.dt.bfloat16
+I32 = mybir.dt.int32
+U32 = mybir.dt.uint32
+U16 = mybir.dt.uint16
+U8 = mybir.dt.uint8
+E2M1X4 = mybir.dt.float4_e2m1fn_x4
+E4M3X4 = mybir.dt.float8_e4m3fn_x4
+E5M2X4 = mybir.dt.float8_e5m2_x4
+COPY = mybir.ActivationFunctionType.Copy
+MAX = mybir.AluOpType.max
+
+P = 128
+PACK = 4
+QUADS = 4
+QUAD = 32
+
+
+def tile_list_weighedpicks_solo_store_plain_kernel(
+    tc, xt_words, xt_scales, w_words, w_scales, sa, sb, vs_words, vs_scales, offs, offs2, offs3, offs4, out
+):
+    nc = tc.nc
+    with ExitStack() as ctx:
+        lists = ctx.enter_context(tc.tile_pool(name="lists", bufs=1))
+        pool = ctx.enter_context(tc.tile_pool(name="work", bufs=1))
+        psum = ctx.enter_context(tc.psum_pool(name="psum", bufs=1))
+
+        idx = lists.tile([P, J // 16], U16, name="idx")
+        idx2 = lists.tile([P, O // 16], U16, name="idx2")
+        idx3 = lists.tile([P, O // 16], U16, name="idx3")
+        idx4 = lists.tile([P, N // 16], U16, name="idx4")
+
+        xw = pool.tile([P, T], U16, name="xw", align_bytes=64)
+        xs = pool.tile([P, T], U8, name="xs", align_bytes=64)
+        ww = pool.tile([P, R], U32, name="ww", align_bytes=64)
+        ws_stage = pool.tile([PACK, QUADS, R // 4], I32, name="ws_stage", align_bytes=64)
+        ws_rows = pool.tile([P, R], U8, name="ws_rows", align_bytes=64)
+        vw = pool.tile([P, S], U32, name="vw", tag="vw", align_bytes=64)
+        vs = pool.tile([P, S], U8, name="vs", tag="vs", align_bytes=64)
+        sa_t = pool.tile([P, PACK], F32, name="sa_t", align_bytes=64)
+        sb_t = pool.tile([P, PACK], F32, name="sb_t", align_bytes=64)
+
+        nc.vector.memset(xs[:].bitcast(I32), 0)
+        nc.vector.memset(ws_rows[:].bitcast(I32), 0)
+        nc.vector.memset(vs[:].bitcast(I32), 0)
+
+        def load_scale_rows(queue, plane, rows, q):
+            queue.dma_start(
+                out=plane[QUAD * q : QUAD * q + 4, :].bitcast(I32),
+                in_=rows[0, 4 * q : 4 * q + 4, :].bitcast(I32),
+            )
+
+        nc.sync.dma_start(idx[:], offs)
+        nc.scalar.dma_start(out=ws_stage[:], in_=w_scales[0].bitcast(I32).rearrange("(q i) c -> i q c", i=4))
+        nc.gpsimd.dma_start(out=sa_t[:], in_=sa.rearrange("(p t) o -> p (t o)", t=PACK))
+        nc.gpsimd.dma_start(out=sb_t[:], in_=sb.rearrange("(p t) o -> p (t o)", t=PACK))
+        load_scale_rows(nc.sync, xs, xt_scales, 0)
+        nc.scalar.dma_start(out=ww[:].bitcast(I32), in_=w_words[0].rearrange("p c t -> p (c t)").bitcast(I32))
+        load_scale_rows(nc.sync, xs, xt_scales, 1)
+        load_scale_rows(nc.scalar, xs, xt_scales, 2)
+        nc.sync.dma_start(out=xw[:].bitcast(I32), in_=xt_words[0].bitcast(I32))
+        load_scale_rows(nc.scalar, xs, xt_scales, 3)
+        nc.sync.dma_start(idx4[:], offs4)
+        nc.sync.dma_start(idx2[:], offs2)
+        nc.sync.dma_start(idx3[:], offs3)
+        load_scale_rows(nc.sync, vs, vs_scales, 0)
+        load_scale_rows(nc.sync, vs, vs_scales, 1)
+        load_scale_rows(nc.sync, vs, vs_scales, 2)
+        load_scale_rows(nc.sync, vs, vs_scales, 3)
+        nc.sync.dma_start(out=vw[:].bitcast(I32), in_=vs_words[0].rearrange("p c t -> p (c t)").bitcast(I32))
+
+        for q in range(QUADS):
+            nc.vector.tensor_copy(out=ws_rows[QUAD * q : QUAD * q + 4, :].bitcast(I32), in_=ws_stage[:, q, :])
+        ws_d = pool.tile([P, PACK, P], U8, name="ws_d", tag="ws_d", align_bytes=64)
+        nc.vector.tensor_copy(out=ws_d[:], in_=ws_rows[:].rearrange("p (c t) -> p t c", t=PACK))
+        xs_g = pool.tile([P, J], U8, name="xs_g", align_bytes=64)
+        nc.vector.tensor_copy(out=xs_g[:], in_=xs[:].indirect(idx[:]))
+        xw_g = pool.tile([P, J], U16, name="xw_g", align_bytes=64)
+        for h in range(2):
+            nc.vector.tensor_copy(out=xw_g[:, h * P : (h + 1) * P], in_=xw[:].indirect(idx[:, 8 * h : 8 * h + 8]))
+        ww_d = pool.tile([P, PACK, P], U32, name="ww_d", align_bytes=64)
+        nc.scalar.copy(out=ww_d[:].rearrange("p t c -> p c t"), in_=ww[:].rearrange("p (c t) -> p c t", t=PACK))
+
+        vs_g = pool.tile([P, N], U8, name="vs_g", align_bytes=64)
+        nc.vector.tensor_copy(out=vs_g[:], in_=vs[:].indirect(idx4[:]))
+
+        ga = [pool.tile([P, 2, O], F32, name="ga%d" % h, align_bytes=64) for h in range(2)]
+        gb = [pool.tile([P, 2, O], F32, name="gb%d" % h, align_bytes=64) for h in range(2)]
+        a_sb = [pool.tile([P, J], F32, name="a%d" % t, tag="vs" if t == 1 else "a%d" % t, align_bytes=64) for t in range(PACK)]
+        for t in range(PACK):
+            pieces = 2 if t == 0 else 1
+            width = J // pieces
+            for h in range(pieces):
+                cols = slice(h * width, (h + 1) * width)
+                a_ps = psum.tile([P, width], F32, name="a_ps%d_%d" % (t, h))
+                nc.tensor.matmul_mx(
+                    out=a_ps[:],
+                    lhsT=ww_d[:, t, :].bitcast(E5M2X4),
+                    lhsT_scale=ws_d[:, t, :],
+                    rhs=xw_g[:, cols].bitcast(E2M1X4),
+                    rhs_scale=xs_g[:, cols],
+                    start=True,
+                    stop=True,
+                )
+                if t == 0:
+                    nc.scalar.copy(out=a_sb[t][:, cols], in_=a_ps[:])
+                else:
+                    nc.vector.tensor_copy(out=a_sb[t][:, cols], in_=a_ps[:])
+            cuts = 2 if t == PACK - 1 else 1
+            places = O // cuts
+            for h in range(cuts):
+                cols = slice(h * places, (h + 1) * places)
+                entries = slice(h * places // 16, (h + 1) * places // 16)
+                nc.scalar.activation(
+                    out=ga[t // 2][:, t % 2, cols], in_=a_sb[t][:].indirect(idx2[:, entries]), func=COPY, scale=sa_t[:, t : t + 1]
+                )
+                nc.scalar.activation(
+                    out=gb[t // 2][:, t % 2, cols], in_=a_sb[t][:].indirect(idx3[:, entries]), func=COPY, scale=sb_t[:, t : t + 1]
+                )
+
+        vw_g = pool.tile([P, N], U32, name="vw_g", align_bytes=64)
+        nc.vector.tensor_copy(out=vw_g[:], in_=vw[:].indirect(idx4[:]))
+        hid = pool.tile([P, O, PACK], BF16, name="hid", tag="vw", align_bytes=64)
+
+        hq = pool.tile([P, O], U32, name="hq", align_bytes=64)
+        hs = pool.tile([P, O], U8, name="hs", align_bytes=64)
+
+        def larger(pair, cols):
+            nc.vector.tensor_tensor(
+                out=hid[:, cols, 2 * pair : 2 * pair + 2],
+                in0=ga[pair][:, :, cols].rearrange("p t o -> p o t"),
+                in1=gb[pair][:, :, cols].rearrange("p t o -> p o t"),
+                op=MAX,
+            )
+
+        larger(0, slice(0, O))
+        halves = [slice(0, O // 2), slice(O // 2, O)]
+        for cols in halves:
+            larger(1, cols)
+            nc.vector.quantize_mx(out=hq[:, cols].bitcast(E5M2X4), scales=hs[:, cols], in_=hid[:, cols, :].rearrange("p o t -> p (o t)"))
+
+        for m in range(N // P):
+            y_ps = psum.tile([P, O], F32, name="y_ps%d" % m)
+            nc.tensor.matmul_mx(
+                out=y_ps[:],
+                lhsT=vw_g[:, m * P : (m + 1) * P].bitcast(E4M3X4),
+                lhsT_scale=vs_g[:, m * P : (m + 1) * P],
+                rhs=hq[:].bitcast(E5M2X4),
+                rhs_scale=hs[:],
+                start=True,
+                stop=True,
+            )
+            y_sb = pool.tile([P, O], F32, name="y%d" % m, align_bytes=64)
+            if m == 0:
+                nc.scalar.copy(out=y_sb[:], in_=y_ps[:])
+                nc.scalar.dma_start(out=out[m * P : (m + 1) * P, :], in_=y_sb[:])
+            else:
+                nc.vector.tensor_copy(out=y_sb[:], in_=y_ps[:])
+                nc.sync.dma_start(out=out[m * P : (m + 1) * P, :], in_=y_sb[:])

@@ -43,7 +43,7 @@ def tile_list_weighedpicks_solo_store_plain_kernel(
         ws_stage = pool.tile([PACK, QUADS, R // 4], I32, name="ws_stage", align_bytes=64)
         ws_rows = pool.tile([P, R], U8, name="ws_rows", align_bytes=64)
         vw = pool.tile([P, S], U32, name="vw", tag="vw", align_bytes=64)
-        vs = pool.tile([P, S], U8, name="vs", tag="vs", align_bytes=64)
+        vs = pool.tile([P, S], U8, name="vs", align_bytes=64)
         sa_t = pool.tile([P, PACK], F32, name="sa_t", align_bytes=64)
         sb_t = pool.tile([P, PACK], F32, name="sb_t", align_bytes=64)
 
@@ -65,11 +65,11 @@ def tile_list_weighedpicks_solo_store_plain_kernel(
         nc.scalar.dma_start(out=ww[:].bitcast(I32), in_=w_words[0].rearrange("p c t -> p (c t)").bitcast(I32))
         load_scale_rows(nc.sync, xs, xt_scales, 1)
         load_scale_rows(nc.scalar, xs, xt_scales, 2)
-        nc.sync.dma_start(out=xw[:].bitcast(I32), in_=xt_words[0].bitcast(I32))
-        load_scale_rows(nc.scalar, xs, xt_scales, 3)
-        nc.sync.dma_start(idx4[:], offs4)
+        load_scale_rows(nc.sync, xs, xt_scales, 3)
+        nc.scalar.dma_start(out=xw[:].bitcast(I32), in_=xt_words[0].bitcast(I32))
         nc.sync.dma_start(idx2[:], offs2)
         nc.sync.dma_start(idx3[:], offs3)
+        nc.sync.dma_start(idx4[:], offs4)
         load_scale_rows(nc.sync, vs, vs_scales, 0)
         load_scale_rows(nc.sync, vs, vs_scales, 1)
         load_scale_rows(nc.sync, vs, vs_scales, 2)
@@ -86,14 +86,15 @@ def tile_list_weighedpicks_solo_store_plain_kernel(
         for h in range(2):
             nc.vector.tensor_copy(out=xw_g[:, h * P : (h + 1) * P], in_=xw[:].indirect(idx[:, 8 * h : 8 * h + 8]))
         ww_d = pool.tile([P, PACK, P], U32, name="ww_d", align_bytes=64)
-        nc.scalar.copy(out=ww_d[:].rearrange("p t c -> p c t"), in_=ww[:].rearrange("p (c t) -> p c t", t=PACK))
+        nc.scalar.copy(
+            out=ww_d[:].rearrange("p t (g i) -> p g t i", i=4),
+            in_=ww[:].rearrange("p (g i t) -> p g t i", i=4, t=PACK),
+        )
 
-        vs_g = pool.tile([P, N], U8, name="vs_g", align_bytes=64)
-        nc.vector.tensor_copy(out=vs_g[:], in_=vs[:].indirect(idx4[:]))
 
         ga = [pool.tile([P, 2, O], F32, name="ga%d" % h, align_bytes=64) for h in range(2)]
         gb = [pool.tile([P, 2, O], F32, name="gb%d" % h, align_bytes=64) for h in range(2)]
-        a_sb = [pool.tile([P, J], F32, name="a%d" % t, tag="vs" if t == 1 else "a%d" % t, align_bytes=64) for t in range(PACK)]
+        a_sb = [pool.tile([P, J], F32, name="a%d" % t, align_bytes=64) for t in range(PACK)]
         for t in range(PACK):
             pieces = 2 if t == 0 else 1
             width = J // pieces
@@ -125,6 +126,8 @@ def tile_list_weighedpicks_solo_store_plain_kernel(
                     out=gb[t // 2][:, t % 2, cols], in_=a_sb[t][:].indirect(idx3[:, entries]), func=COPY, scale=sb_t[:, t : t + 1]
                 )
 
+        vs_g = pool.tile([P, N], U8, name="vs_g", align_bytes=64)
+        nc.vector.tensor_copy(out=vs_g[:], in_=vs[:].indirect(idx4[:]))
         vw_g = pool.tile([P, N], U32, name="vw_g", align_bytes=64)
         nc.vector.tensor_copy(out=vw_g[:], in_=vw[:].indirect(idx4[:]))
         hid = pool.tile([P, O, PACK], BF16, name="hid", tag="vw", align_bytes=64)

@@ -61,12 +61,12 @@ def tile_list_weighedpicks_solo_store_plain_kernel(
         nc.scalar.dma_start(out=ws_stage[:], in_=w_scales[0].bitcast(I32).rearrange("(q i) c -> i q c", i=4))
         nc.gpsimd.dma_start(out=sa_t[:], in_=sa.rearrange("(p t) o -> p (t o)", t=PACK))
         nc.gpsimd.dma_start(out=sb_t[:], in_=sb.rearrange("(p t) o -> p (t o)", t=PACK))
-        load_scale_rows(nc.sync, xs, xt_scales, 0)
-        nc.scalar.dma_start(out=ww[:].bitcast(I32), in_=w_words[0].rearrange("p c t -> p (c t)").bitcast(I32))
-        load_scale_rows(nc.sync, xs, xt_scales, 1)
+        nc.sync.dma_start(out=xw[:].bitcast(I32), in_=xt_words[0].bitcast(I32))
         load_scale_rows(nc.scalar, xs, xt_scales, 2)
-        load_scale_rows(nc.sync, xs, xt_scales, 3)
-        nc.scalar.dma_start(out=xw[:].bitcast(I32), in_=xt_words[0].bitcast(I32))
+        load_scale_rows(nc.sync, xs, xt_scales, 0)
+        load_scale_rows(nc.scalar, xs, xt_scales, 3)
+        load_scale_rows(nc.sync, xs, xt_scales, 1)
+        nc.scalar.dma_start(out=ww[:].bitcast(I32), in_=w_words[0].rearrange("p c t -> p (c t)").bitcast(I32))
         nc.sync.dma_start(idx2[:], offs2)
         nc.sync.dma_start(idx3[:], offs3)
         nc.sync.dma_start(idx4[:], offs4)
@@ -79,17 +79,19 @@ def tile_list_weighedpicks_solo_store_plain_kernel(
         for q in range(QUADS):
             nc.vector.tensor_copy(out=ws_rows[QUAD * q : QUAD * q + 4, :].bitcast(I32), in_=ws_stage[:, q, :])
         ws_d = pool.tile([P, PACK, P], U8, name="ws_d", tag="ws_d", align_bytes=64)
-        nc.vector.tensor_copy(out=ws_d[:], in_=ws_rows[:].rearrange("p (c t) -> p t c", t=PACK))
+        ws_by_slot = ws_rows[:].rearrange("p (c t) -> p t c", t=PACK)
+        nc.gpsimd.tensor_copy(out=ws_d[:, 0, :], in_=ws_by_slot[:, 0, :])
+        nc.gpsimd.tensor_copy(out=ws_d[:, 1:, :], in_=ws_by_slot[:, 1:, :])
         xs_g = pool.tile([P, J], U8, name="xs_g", align_bytes=64)
-        nc.vector.tensor_copy(out=xs_g[:], in_=xs[:].indirect(idx[:]))
         xw_g = pool.tile([P, J], U16, name="xw_g", align_bytes=64)
+        nc.vector.tensor_copy(out=xw_g[:], in_=xw[:].indirect(idx[:]))
         for h in range(2):
-            nc.vector.tensor_copy(out=xw_g[:, h * P : (h + 1) * P], in_=xw[:].indirect(idx[:, 8 * h : 8 * h + 8]))
+            nc.vector.tensor_copy(out=xs_g[:, h * P : (h + 1) * P], in_=xs[:].indirect(idx[:, 8 * h : 8 * h + 8]))
         ww_d = pool.tile([P, PACK, P], U32, name="ww_d", align_bytes=64)
-        nc.scalar.copy(
-            out=ww_d[:].rearrange("p t (g i) -> p g t i", i=4),
-            in_=ww[:].rearrange("p (g i t) -> p g t i", i=4, t=PACK),
-        )
+        ww_by_slot = ww[:].rearrange("p (g i t) -> p g t i", i=4, t=PACK)
+        ww_dealt = ww_d[:].rearrange("p t (g i) -> p g t i", i=4)
+        nc.scalar.copy(out=ww_dealt[:, :, 0, :], in_=ww_by_slot[:, :, 0, :])
+        nc.scalar.copy(out=ww_dealt[:, :, 1:, :], in_=ww_by_slot[:, :, 1:, :])
 
 
         ga = [pool.tile([P, 2, O], F32, name="ga%d" % h, align_bytes=64) for h in range(2)]

from contextlib import ExitStack

import concourse.mybir as mybir

K, T, J, R, O, N, S = 512, 1024, 256, 512, 128, 256, 1024
FLOPS = 2 * K * R * J + 2 * R * N * O

F32 = mybir.dt.float32
BF16 = mybir.dt.bfloat16
I32 = mybir.dt.int32
U32 = mybir.dt.uint32
U16 = mybir.dt.uint16
U8 = mybir.dt.uint8
E2M1X4 = mybir.dt.float4_e2m1fn_x4
E4M3X4 = mybir.dt.float8_e4m3fn_x4
E5M2X4 = mybir.dt.float8_e5m2_x4
COPY = mybir.ActivationFunctionType.Copy
MAX = mybir.AluOpType.max

P = 128
PACK = 4
QUADS = 4
QUAD = 32


def tile_list_weighedpicks_solo_store_plain_kernel(
    tc, xt_words, xt_scales, w_words, w_scales, sa, sb, vs_words, vs_scales, offs, offs2, offs3, offs4, out
):
    nc = tc.nc
    with ExitStack() as ctx:
        lists = ctx.enter_context(tc.tile_pool(name="lists", bufs=1))
        pool = ctx.enter_context(tc.tile_pool(name="work", bufs=1))
        psum = ctx.enter_context(tc.psum_pool(name="psum", bufs=1))

        idx = lists.tile([P, J // 16], U16, name="idx")
        idx2 = lists.tile([P, O // 16], U16, name="idx2")
        idx3 = lists.tile([P, O // 16], U16, name="idx3")
        idx4 = lists.tile([P, N // 16], U16, name="idx4")

        xw = pool.tile([P, T], U16, name="xw", align_bytes=64)
        xs = pool.tile([P, T], U8, name="xs", align_bytes=64)
        ww = pool.tile([P, R], U32, name="ww", align_bytes=64)
        ws_stage = pool.tile([PACK, QUADS, R // 4], I32, name="ws_stage", align_bytes=64)
        ws_rows = pool.tile([P, R], U8, name="ws_rows", align_bytes=64)
        vw = pool.tile([P, S], U32, name="vw", tag="vw", align_bytes=64)
        vs = pool.tile([P, S], U8, name="vs", align_bytes=64)
        sa_t = pool.tile([P, PACK], F32, name="sa_t", align_bytes=64)
        sb_t = pool.tile([P, PACK], F32, name="sb_t", align_bytes=64)

        nc.vector.memset(xs[:].bitcast(I32), 0)
        nc.vector.memset(ws_rows[:].bitcast(I32), 0)
        nc.vector.memset(vs[:].bitcast(I32), 0)

        def load_scale_rows(queue, plane, rows, q):
            queue.dma_start(
                out=plane[QUAD * q : QUAD * q + 4, :].bitcast(I32),
                in_=rows[0, 4 * q : 4 * q + 4, :].bitcast(I32),
            )

        nc.sync.dma_start(idx[:], offs)
        nc.scalar.dma_start(out=ws_stage[:], in_=w_scales[0].bitcast(I32).rearrange("(q i) c -> i q c", i=4))
        nc.gpsimd.dma_start(out=sa_t[:], in_=sa.rearrange("(p t) o -> p (t o)", t=PACK))
        nc.gpsimd.dma_start(out=sb_t[:], in_=sb.rearrange("(p t) o -> p (t o)", t=PACK))
        nc.sync.dma_start(out=xw[:].bitcast(I32), in_=xt_words[0].bitcast(I32))
        load_scale_rows(nc.scalar, xs, xt_scales, 2)
        load_scale_rows(nc.sync, xs, xt_scales, 0)
        load_scale_rows(nc.scalar, xs, xt_scales, 3)
        load_scale_rows(nc.sync, xs, xt_scales, 1)
        nc.scalar.dma_start(out=ww[:].bitcast(I32), in_=w_words[0].rearrange("p c t -> p (c t)").bitcast(I32))
        nc.sync.dma_start(idx2[:], offs2)
        nc.sync.dma_start(idx3[:], offs3)
        nc.sync.dma_start(idx4[:], offs4)
        load_scale_rows(nc.sync, vs, vs_scales, 0)
        load_scale_rows(nc.sync, vs, vs_scales, 1)
        load_scale_rows(nc.sync, vs, vs_scales, 2)
        load_scale_rows(nc.sync, vs, vs_scales, 3)
        nc.sync.dma_start(out=vw[:].bitcast(I32), in_=vs_words[0].rearrange("p c t -> p (c t)").bitcast(I32))

        for q in range(QUADS):
            nc.vector.tensor_copy(out=ws_rows[QUAD * q : QUAD * q + 4, :].bitcast(I32), in_=ws_stage[:, q, :])
        ws_d = pool.tile([P, PACK, P], U8, name="ws_d", tag="ws_d", align_bytes=64)
        ws_by_slot = ws_rows[:].rearrange("p (c t) -> p t c", t=PACK)
        nc.gpsimd.tensor_copy(out=ws_d[:, 0, :], in_=ws_by_slot[:, 0, :])
        nc.gpsimd.tensor_copy(out=ws_d[:, 1:, :], in_=ws_by_slot[:, 1:, :])
        xs_g = pool.tile([P, J], U8, name="xs_g", align_bytes=64)
        xw_g = pool.tile([P, J], U16, name="xw_g", align_bytes=64)
        nc.vector.tensor_copy(out=xw_g[:], in_=xw[:].indirect(idx[:]))
        for h in range(2):
            nc.vector.tensor_copy(out=xs_g[:, h * P : (h + 1) * P], in_=xs[:].indirect(idx[:, 8 * h : 8 * h + 8]))
        ww_d = pool.tile([P, PACK, P], U32, name="ww_d", align_bytes=64)
        ww_by_slot = ww[:].rearrange("p (g i t) -> p g t i", i=4, t=PACK)
        ww_dealt = ww_d[:].rearrange("p t (g i) -> p g t i", i=4)
        nc.scalar.copy(out=ww_dealt[:, :, 0, :], in_=ww_by_slot[:, :, 0, :])
        nc.scalar.copy(out=ww_dealt[:, :, 1:, :], in_=ww_by_slot[:, :, 1:, :])


        ga = [pool.tile([P, 2, O], F32, name="ga%d" % h, align_bytes=64) for h in range(2)]
        gb = [pool.tile([P, 2, O], F32, name="gb%d" % h, align_bytes=64) for h in range(2)]
        a_sb = [pool.tile([P, J], F32, name="a%d" % t, align_bytes=64) for t in range(PACK)]
        for t in range(PACK):
            pieces = 2 if t == 0 else 1
            width = J // pieces
            for h in range(pieces):
                cols = slice(h * width, (h + 1) * width)
                a_ps = psum.tile([P, width], F32, name="a_ps%d_%d" % (t, h))
                nc.tensor.matmul_mx(
                    out=a_ps[:],
                    lhsT=ww_d[:, t, :].bitcast(E5M2X4),
                    lhsT_scale=ws_d[:, t, :],
                    rhs=xw_g[:, cols].bitcast(E2M1X4),
                    rhs_scale=xs_g[:, cols],
                    start=True,
                    stop=True,
                )
                if t == 0:
                    nc.scalar.copy(out=a_sb[t][:, cols], in_=a_ps[:])
                else:
                    nc.vector.tensor_copy(out=a_sb[t][:, cols], in_=a_ps[:])
            cuts = 2 if t == PACK - 1 else 1
            places = O // cuts
            for h in range(cuts):
                cols = slice(h * places, (h + 1) * places)
                entries = slice(h * places // 16, (h + 1) * places // 16)
                nc.scalar.activation(
                    out=ga[t // 2][:, t % 2, cols], in_=a_sb[t][:].indirect(idx2[:, entries]), func=COPY, scale=sa_t[:, t : t + 1]
                )
                nc.scalar.activation(
                    out=gb[t // 2][:, t % 2, cols], in_=a_sb[t][:].indirect(idx3[:, entries]), func=COPY, scale=sb_t[:, t : t + 1]
                )

        vs_g = pool.tile([P, N], U8, name="vs_g", align_bytes=64)
        nc.vector.tensor_copy(out=vs_g[:], in_=vs[:].indirect(idx4[:]))
        vw_g = pool.tile([P, N], U32, name="vw_g", align_bytes=64)
        nc.vector.tensor_copy(out=vw_g[:], in_=vw[:].indirect(idx4[:]))
        hid = pool.tile([P, O, PACK], BF16, name="hid", tag="vw", align_bytes=64)

        hq = pool.tile([P, O], U32, name="hq", align_bytes=64)
        hs = pool.tile([P, O], U8, name="hs", align_bytes=64)

        def larger(pair, cols):
            nc.vector.tensor_tensor(
                out=hid[:, cols, 2 * pair : 2 * pair + 2],
                in0=ga[pair][:, :, cols].rearrange("p t o -> p o t"),
                in1=gb[pair][:, :, cols].rearrange("p t o -> p o t"),
                op=MAX,
            )

        larger(0, slice(0, O))
        halves = [slice(0, O // 2), slice(O // 2, O)]
        for cols in halves:
            larger(1, cols)
            nc.vector.quantize_mx(out=hq[:, cols].bitcast(E5M2X4), scales=hs[:, cols], in_=hid[:, cols, :].rearrange("p o t -> p (o t)"))

        for m in range(N // P):
            y_ps = psum.tile([P, O], F32, name="y_ps%d" % m)
            nc.tensor.matmul_mx(
                out=y_ps[:],
                lhsT=vw_g[:, m * P : (m + 1) * P].bitcast(E4M3X4),
                lhsT_scale=vs_g[:, m * P : (m + 1) * P],
                rhs=hq[:].bitcast(E5M2X4),
                rhs_scale=hs[:],
                start=True,
                stop=True,
            )
            y_sb = pool.tile([P, O], F32, name="y%d" % m, align_bytes=64)
            if m == 0:
                nc.scalar.copy(out=y_sb[:], in_=y_ps[:])
                nc.scalar.dma_start(out=out[m * P : (m + 1) * P, :], in_=y_sb[:])
            else:
                nc.vector.tensor_copy(out=y_sb[:], in_=y_ps[:])
                nc.sync.dma_start(out=out[m * P : (m + 1) * P, :], in_=y_sb[:])
